import numpy as np, ml_dtypes
CORES = [1,2,5,7,57,58,61,63,73,74,77,79]
N = 12
R, TK = 64, 64
def setup_inputs(rng):
    u = (rng.standard_normal((N, 128, R), dtype=np.float32) / 11).astype(ml_dtypes.bfloat16)
    return {"x": rng.standard_normal((N, 128, TK), dtype=np.float32).astype(ml_dtypes.bfloat16), "u": u, "ut": u.transpose(0, 2, 1).copy(), "vt": rng.standard_normal((N, R, 128), dtype=np.float32).astype(ml_dtypes.bfloat16)}
def setup_inputs_big(rng):
    d = setup_inputs(rng)
    for k in ("x", "u", "ut", "vt"): d[k] = (d[k].astype(np.float32) * 1024.0).astype(d[k].dtype)
    return d
def setup_inputs_small(rng):
    d = setup_inputs(rng)
    for k in ("x", "u", "ut", "vt"): d[k] = (d[k].astype(np.float32) * (1 / 1024.0)).astype(d[k].dtype)
    return d
def setup_inputs_apart(rng):
    d = setup_inputs(rng)
    f = (10.0 ** rng.permutation(np.linspace(-1.5, 1.5, N))).astype(np.float32).reshape(N, 1, 1)
    for k in ("x", "u", "ut", "vt"): d[k] = (d[k].astype(np.float32) * f).astype(d[k].dtype)
    return d
def tie_inputs(x):
    x = dict(x)
    x["ut"] = x["u"].transpose(0, 2, 1).copy()
    return x
def reference(x, u, ut, vt):
    X, U, VT = x.astype(np.float64), u.astype(np.float64), vt.astype(np.float64)
    y = np.stack([sum(VT[j].T @ (U[j].T @ X[r]) for j in range(N)) for r in range(N)])
    return {"y": y.astype(ml_dtypes.bfloat16 if x.dtype != np.float64 else np.float64)}

@@ -1,0 +1,109 @@
+from concourse.bass import DstId, RemoteDMATransfer
+
+SCRATCH = {
+    "fb": ("sbuf", [128, 256], "bfloat16"),
+    "la0": ("sbuf", [128, 256], "bfloat16"),
+    "la1": ("sbuf", [128, 256], "bfloat16"),
+    "la2": ("sbuf", [128, 256], "bfloat16"),
+    "la3": ("sbuf", [128, 256], "bfloat16"),
+    "xs": ("sbuf", [128, 64], "bfloat16"),
+    "mc": ("sbuf", [128, 128], "bfloat16"),
+    "rA": ("sbuf", [128, 128], "bfloat16"),
+    "rB": ("sbuf", [128, 128], "bfloat16"),
+    "ys": ("sbuf", [128, 64], "bfloat16"),
+    "pm": ("psum", [128, 512], "float32"),
+    "py": ("psum", [128, 512], "float32"),
+}
+SEMAPHORES = ["ld", "lx", "ms", "f0", "f1", "f2", "f3", "mm", "cp", "own", "oA", "oB", "my", "cy", "st", "snt"]
+
+N_OWN = 4
+
+
+def _take(mask, n):
+    bits = [b for b in range(mask.bit_length()) if (mask >> b) & 1][:n]
+    return sum(1 << b for b in bits)
+
+
+def _count(mask):
+    return sum((mask >> b) & 1 for b in range(mask.bit_length()))
+
+
+def rank_program(g, core, T, topo):
+    if T.rank_of(core) is None:
+        return
+    S = T.sem
+    ranks = list(T.cores)
+    chips = sorted({topo.chip(c) for c in ranks})
+    here = [c for c in ranks if topo.chip(c) == topo.chip(core)]
+    ports = sorted((c for c in here if all(topo.may_write(c, d) for d in ranks if d != c)), key=topo.die)
+    me = here.index(core)
+    is_port = core in ports
+
+    def dst(c):
+        rid, pid, _ = topo.addr(c)
+        return DstId(rid=rid, pnc=pid)
+
+    away = [c for c in ranks if c not in here]
+    m_off = topo.mask(core, away[0])
+    m_on = topo.mask(core, [c for c in here if c != core][0]) & ~m_off
+    n_off = _count(m_off)
+
+    g.sync.dma_start(T.fb[0:64, 0:128], T.ut[:, :]).then_inc(S.ld, 16)
+    g.scalar.dma_start(T.fb[0:64, 128:256], T.vt[:, :]).then_inc(S.ld, 16)
+    g.vector.memset(T.fb[64:128, :], 0).then_inc(S.ms, 1)
+    g.sync.dma_start(T.xs[:, :], T.x[:, :]).then_inc(S.lx, 16)
+
+    to = [p for p in ports if p != core]
+    g.wait_ge(S.ld, 32)
+    g.wait_ge(S.ms, 1)
+    g.remote_dma_fused(
+        [RemoteDMATransfer(dst_ids=[dst(p) for p in to], dma_engine_mask=m_off, remote_sem=S["f%d" % me],
+                           srcs=[T.fb[:, :]], dsts=[T["la%d" % me][:, :] for _ in to])],
+        local_sem=S.snt)
+    sent = n_off
+
+    if is_port:
+        g.tensor.wait_ge(S.ld, 32)
+        g.tensor.matmul(T.pm[:, 0:128], T.fb[0:64, 0:128], T.fb[0:64, 128:256], True, False)
+        others = [here.index(p) for p in to] + [k for k, c in enumerate(here) if c not in ports]
+        for i, k in enumerate(others):
+            la = T["la%d" % k]
+            g.tensor.wait_ge(S["f%d" % k], n_off)
+            mmul = g.tensor.matmul(T.pm[:, 0:128], la[0:64, 0:128], la[0:64, 128:256], False, i == len(others) - 1)
+        mmul.then_inc(S.mm, 1)
+        g.vector.wait_ge(S.mm, 1)
+        g.vector.tensor_copy(T.mc[:, :], T.pm[:, 0:128]).then_inc(S.cp, 1)
+
+        q = ports.index(core)
+        target = chips[(chips.index(topo.chip(core)) + 1 + q) % len(chips)]
+        far = [c for c in ranks if topo.chip(c) == target]
+        name = "AB"[q]
+        g.wait_ge(S.cp, 1)
+        g.remote_dma_fused(
+            [RemoteDMATransfer(dst_ids=[dst(c) for c in far], dma_engine_mask=m_off, remote_sem=S["o" + name],
+                               srcs=[T.mc[:, :]], dsts=[T["r" + name][:, :] for _ in far])],
+            local_sem=S.snt)
+        sent += n_off
+        plain = [c for c in here if c not in ports and topo.die(c) == topo.die(core)]
+        m_own = _take(m_on, N_OWN)
+        g.remote_dma_fused(
+            [RemoteDMATransfer(dst_ids=[dst(c) for c in plain], dma_engine_mask=m_own, remote_sem=S.own,
+                               srcs=[T.mc[:, :]], dsts=[T.mc[:, :] for _ in plain])],
+            local_sem=S.snt)
+        sent += N_OWN
+        g.tensor.wait_ge(S.cp, 1)
+    else:
+        g.tensor.wait_ge(S.own, N_OWN)
+
+    g.tensor.wait_ge(S.lx, 16)
+    g.tensor.matmul(T.py[:, 0:64], T.mc[:, :], T.xs[:, :], True, False)
+    g.tensor.wait_ge(S.oA, n_off)
+    g.tensor.matmul(T.py[:, 0:64], T.rA[:, :], T.xs[:, :], False, False)
+    g.tensor.wait_ge(S.oB, n_off)
+    g.tensor.matmul(T.py[:, 0:64], T.rB[:, :], T.xs[:, :], False, True).then_inc(S.my, 1)
+    g.vector.wait_ge(S.my, 1)
+    g.vector.tensor_copy(T.ys[:, :], T.py[:, 0:64]).then_inc(S.cy, 1)
+    g.sync.wait_ge(S.cy, 1)
+    g.sync.dma_start(T.y[:, :], T.ys[:, :]).then_inc(S.st, 16)
+    g.sync.wait_ge(S.st, 16)
+    g.wait_ge(S.snt, sent)

@@ -11,21 +11,21 @@ SCRATCH = {
     "rA": ("sbuf", [128, 128], "bfloat16"),
     "rB": ("sbuf", [128, 128], "bfloat16"),
     "ys": ("sbuf", [128, 64], "bfloat16"),
-    "pm": ("psum", [128, 512], "float32"),
+    "pm0": ("psum", [128, 512], "float32"),
+    "pm1": ("psum", [128, 512], "float32"),
     "py": ("psum", [128, 512], "float32"),
 }
-SEMAPHORES = ["ld", "lx", "ms", "f0", "f1", "f2", "f3", "mm", "cp", "own", "oA", "oB", "my", "cy", "st", "snt"]
+SEMAPHORES = ["ld", "lx", "ms", "f0", "f1", "f2", "f3", "mm0", "mm1", "cp", "own", "oA", "oB", "my", "cy", "st", "snt"]
 
 N_OWN = 4
 
 
-def _take(mask, n):
-    bits = [b for b in range(mask.bit_length()) if (mask >> b) & 1][:n]
+def _bits(mask):
+    return [b for b in range(mask.bit_length()) if (mask >> b) & 1]
+
+
+def _mask_of(bits):
     return sum(1 << b for b in bits)
-
-
-def _count(mask):
-    return sum((mask >> b) & 1 for b in range(mask.bit_length()))
 
 
 def rank_program(g, core, T, topo):
@@ -34,73 +34,97 @@ def rank_program(g, core, T, topo):
     S = T.sem
     ranks = list(T.cores)
     chips = sorted({topo.chip(c) for c in ranks})
-    here = [c for c in ranks if topo.chip(c) == topo.chip(core)]
-    ports = sorted((c for c in here if all(topo.may_write(c, d) for d in ranks if d != c)), key=topo.die)
-    me = here.index(core)
-    is_port = core in ports
+
+    def on(ch):
+        return [c for c in ranks if topo.chip(c) == ch]
+
+    def ports_of(ch):
+        return sorted((c for c in on(ch) if all(topo.may_write(c, d) for d in ranks if d != c)), key=topo.die)
 
     def dst(c):
         rid, pid, _ = topo.addr(c)
         return DstId(rid=rid, pnc=pid)
 
+    mine = topo.chip(core)
+    here = on(mine)
+    ports = ports_of(mine)
+    me = here.index(core)
+    is_port = core in ports
+    my_die = topo.die(core)
+    q = [topo.die(p) for p in ports].index(my_die)
+    near, other = "AB"[q], "AB"[1 - q]
+
     away = [c for c in ranks if c not in here]
     m_off = topo.mask(core, away[0])
     m_on = topo.mask(core, [c for c in here if c != core][0]) & ~m_off
-    n_off = _count(m_off)
+    n_off = len(_bits(m_off))
+    n_on = len(_bits(m_on))
+    sent = 0
+
+    def write(src, to, buf, sem, mask):
+        g.remote_dma_fused(
+            [RemoteDMATransfer(dst_ids=[dst(c) for c in to], dma_engine_mask=mask, remote_sem=sem,
+                               srcs=[src[:, :]], dsts=[buf[:, :] for _ in to])],
+            local_sem=S.snt)
+        return len(_bits(mask))
 
     g.sync.dma_start(T.fb[0:64, 0:128], T.ut[:, :]).then_inc(S.ld, 16)
     g.scalar.dma_start(T.fb[0:64, 128:256], T.vt[:, :]).then_inc(S.ld, 16)
     g.vector.memset(T.fb[64:128, :], 0).then_inc(S.ms, 1)
     g.sync.dma_start(T.xs[:, :], T.x[:, :]).then_inc(S.lx, 16)
 
-    to = [p for p in ports if p != core]
     g.wait_ge(S.ld, 32)
     g.wait_ge(S.ms, 1)
-    g.remote_dma_fused(
-        [RemoteDMATransfer(dst_ids=[dst(p) for p in to], dma_engine_mask=m_off, remote_sem=S["f%d" % me],
-                           srcs=[T.fb[:, :]], dsts=[T["la%d" % me][:, :] for _ in to])],
-        local_sem=S.snt)
-    sent = n_off
+    for p in sorted((p for p in ports if p != core), key=lambda p: topo.die(p) != my_die):
+        sent += write(T.fb, [p], T["la%d" % me], S["f%d" % me], m_off if is_port or topo.die(p) == my_die else m_on)
 
     if is_port:
+        plains = sorted((c for c in here if c not in ports), key=lambda c: topo.die(c) != my_die)
+        order = [(T.fb, None, 0)]
+        order += [(T["la%d" % here.index(c)], S["f%d" % here.index(c)],
+                   n_off if c in ports or topo.die(c) == my_die else n_on) for c in [p for p in ports if p != core] + plains]
         g.tensor.wait_ge(S.ld, 32)
-        g.tensor.matmul(T.pm[:, 0:128], T.fb[0:64, 0:128], T.fb[0:64, 128:256], True, False)
-        others = [here.index(p) for p in to] + [k for k, c in enumerate(here) if c not in ports]
-        for i, k in enumerate(others):
-            la = T["la%d" % k]
-            g.tensor.wait_ge(S["f%d" % k], n_off)
-            mmul = g.tensor.matmul(T.pm[:, 0:128], la[0:64, 0:128], la[0:64, 128:256], False, i == len(others) - 1)
-        mmul.then_inc(S.mm, 1)
-        g.vector.wait_ge(S.mm, 1)
-        g.vector.tensor_copy(T.mc[:, :], T.pm[:, 0:128]).then_inc(S.cp, 1)
+        for i, (buf, sem, cnt) in enumerate(order):
+            if sem is not None:
+                g.tensor.wait_ge(sem, cnt)
+            last = i == len(order) - 1
+            for h in range(2):
+                mmul = g.tensor.matmul(T["pm%d" % h][:, 0:64], buf[0:64, 0:128], buf[0:64, 128 + 64 * h:192 + 64 * h],
+                                       i == 0, last)
+                if last:
+                    mmul.then_inc(S["mm%d" % h], 1)
+        for h in range(2):
+            g.vector.wait_ge(S["mm%d" % h], 1)
+            g.vector.tensor_copy(T.mc[:, 64 * h:64 * h + 64], T["pm%d" % h][:, 0:64]).then_inc(S.cp, 1)
 
-        q = ports.index(core)
-        target = chips[(chips.index(topo.chip(core)) + 1 + q) % len(chips)]
-        far = [c for c in ranks if topo.chip(c) == target]
-        name = "AB"[q]
-        g.wait_ge(S.cp, 1)
-        g.remote_dma_fused(
-            [RemoteDMATransfer(dst_ids=[dst(c) for c in far], dma_engine_mask=m_off, remote_sem=S["o" + name],
-                               srcs=[T.mc[:, :]], dsts=[T["r" + name][:, :] for _ in far])],
-            local_sem=S.snt)
-        sent += n_off
-        plain = [c for c in here if c not in ports and topo.die(c) == topo.die(core)]
-        m_own = _take(m_on, N_OWN)
-        g.remote_dma_fused(
-            [RemoteDMATransfer(dst_ids=[dst(c) for c in plain], dma_engine_mask=m_own, remote_sem=S.own,
-                               srcs=[T.mc[:, :]], dsts=[T.mc[:, :] for _ in plain])],
-            local_sem=S.snt)
-        sent += N_OWN
-        g.tensor.wait_ge(S.cp, 1)
+        target = chips[(chips.index(mine) + 1 + q) % len(chips)]
+        far = on(target)
+        far_ports = ports_of(target)
+        first = [c for c in far if c not in far_ports and topo.die(c) == my_die]
+        rest = [c for c in far if topo.die(c) != my_die]
+        g.wait_ge(S.cp, 2)
+        sent += write(T.mc, first, T["r" + near], S["o" + near], m_off)
+        sent += write(T.mc, rest, T["r" + near], S["o" + near], m_off)
+        sent += write(T.mc, [c for c in here if c not in ports and topo.die(c) == my_die], T.mc, S.own,
+                      _mask_of(_bits(m_on)[:N_OWN]))
+        g.tensor.wait_ge(S.cp, 2)
+        due = ["mc", other, near]
     else:
-        g.tensor.wait_ge(S.own, N_OWN)
+        g.wait_ge(S["o" + near], n_off)
+        sent += write(T["r" + near], [p for p in ports if topo.die(p) == my_die], T["r" + near], S["o" + near], m_off | m_on)
+        due = [near, "mc", other]
 
     g.tensor.wait_ge(S.lx, 16)
-    g.tensor.matmul(T.py[:, 0:64], T.mc[:, :], T.xs[:, :], True, False)
-    g.tensor.wait_ge(S.oA, n_off)
-    g.tensor.matmul(T.py[:, 0:64], T.rA[:, :], T.xs[:, :], False, False)
-    g.tensor.wait_ge(S.oB, n_off)
-    g.tensor.matmul(T.py[:, 0:64], T.rB[:, :], T.xs[:, :], False, True).then_inc(S.my, 1)
+    for i, m in enumerate(due):
+        if m == "mc":
+            if not is_port:
+                g.tensor.wait_ge(S.own, N_OWN)
+            mat = T.mc
+        else:
+            g.tensor.wait_ge(S["o" + m], n_off + n_on if is_port and m == near else n_off)
+            mat = T["r" + m]
+        mmul = g.tensor.matmul(T.py[:, 0:64], mat[:, :], T.xs[:, :], i == 0, i == len(due) - 1)
+    mmul.then_inc(S.my, 1)
     g.vector.wait_ge(S.my, 1)
     g.vector.tensor_copy(T.ys[:, :], T.py[:, 0:64]).then_inc(S.cy, 1)
     g.sync.wait_ge(S.cy, 1)

from concourse.bass import DstId, RemoteDMATransfer

SCRATCH = {
    "fb": ("sbuf", [128, 256], "bfloat16"),
    "la0": ("sbuf", [128, 256], "bfloat16"),
    "la1": ("sbuf", [128, 256], "bfloat16"),
    "la2": ("sbuf", [128, 256], "bfloat16"),
    "la3": ("sbuf", [128, 256], "bfloat16"),
    "xs": ("sbuf", [128, 64], "bfloat16"),
    "mc": ("sbuf", [128, 128], "bfloat16"),
    "rA": ("sbuf", [128, 128], "bfloat16"),
    "rB": ("sbuf", [128, 128], "bfloat16"),
    "ys": ("sbuf", [128, 64], "bfloat16"),
    "pm0": ("psum", [128, 512], "float32"),
    "pm1": ("psum", [128, 512], "float32"),
    "py": ("psum", [128, 512], "float32"),
}
SEMAPHORES = ["ld", "lx", "ms", "f0", "f1", "f2", "f3", "mm0", "mm1", "cp", "own", "oA", "oB", "my", "cy", "st", "snt"]

N_OWN = 4


def _bits(mask):
    return [b for b in range(mask.bit_length()) if (mask >> b) & 1]


def _mask_of(bits):
    return sum(1 << b for b in bits)


def rank_program(g, core, T, topo):
    if T.rank_of(core) is None:
        return
    S = T.sem
    ranks = list(T.cores)
    chips = sorted({topo.chip(c) for c in ranks})

    def on(ch):
        return [c for c in ranks if topo.chip(c) == ch]

    def ports_of(ch):
        return sorted((c for c in on(ch) if all(topo.may_write(c, d) for d in ranks if d != c)), key=topo.die)

    def dst(c):
        rid, pid, _ = topo.addr(c)
        return DstId(rid=rid, pnc=pid)

    mine = topo.chip(core)
    here = on(mine)
    ports = ports_of(mine)
    me = here.index(core)
    is_port = core in ports
    my_die = topo.die(core)
    q = [topo.die(p) for p in ports].index(my_die)
    near, other = "AB"[q], "AB"[1 - q]

    away = [c for c in ranks if c not in here]
    m_off = topo.mask(core, away[0])
    m_on = topo.mask(core, [c for c in here if c != core][0]) & ~m_off
    n_off = len(_bits(m_off))
    n_on = len(_bits(m_on))
    sent = 0

    def write(src, to, buf, sem, mask):
        g.remote_dma_fused(
            [RemoteDMATransfer(dst_ids=[dst(c) for c in to], dma_engine_mask=mask, remote_sem=sem,
                               srcs=[src[:, :]], dsts=[buf[:, :] for _ in to])],
            local_sem=S.snt)
        return len(_bits(mask))

    g.sync.dma_start(T.fb[0:64, 0:128], T.ut[:, :]).then_inc(S.ld, 16)
    g.scalar.dma_start(T.fb[0:64, 128:256], T.vt[:, :]).then_inc(S.ld, 16)
    g.vector.memset(T.fb[64:128, :], 0).then_inc(S.ms, 1)
    g.sync.dma_start(T.xs[:, :], T.x[:, :]).then_inc(S.lx, 16)

    g.wait_ge(S.ld, 32)
    g.wait_ge(S.ms, 1)
    for p in sorted((p for p in ports if p != core), key=lambda p: topo.die(p) != my_die):
        sent += write(T.fb, [p], T["la%d" % me], S["f%d" % me], m_off if is_port or topo.die(p) == my_die else m_on)

    if is_port:
        plains = sorted((c for c in here if c not in ports), key=lambda c: topo.die(c) != my_die)
        order = [(T.fb, None, 0)]
        order += [(T["la%d" % here.index(c)], S["f%d" % here.index(c)],
                   n_off if c in ports or topo.die(c) == my_die else n_on) for c in [p for p in ports if p != core] + plains]
        g.tensor.wait_ge(S.ld, 32)
        for i, (buf, sem, cnt) in enumerate(order):
            if sem is not None:
                g.tensor.wait_ge(sem, cnt)
            last = i == len(order) - 1
            for h in range(2):
                mmul = g.tensor.matmul(T["pm%d" % h][:, 0:64], buf[0:64, 0:128], buf[0:64, 128 + 64 * h:192 + 64 * h],
                                       i == 0, last)
                if last:
                    mmul.then_inc(S["mm%d" % h], 1)
        for h in range(2):
            g.vector.wait_ge(S["mm%d" % h], 1)
            g.vector.tensor_copy(T.mc[:, 64 * h:64 * h + 64], T["pm%d" % h][:, 0:64]).then_inc(S.cp, 1)

        target = chips[(chips.index(mine) + 1 + q) % len(chips)]
        far = on(target)
        far_ports = ports_of(target)
        first = [c for c in far if c not in far_ports and topo.die(c) == my_die]
        rest = [c for c in far if topo.die(c) != my_die]
        g.wait_ge(S.cp, 2)
        sent += write(T.mc, first, T["r" + near], S["o" + near], m_off)
        sent += write(T.mc, rest, T["r" + near], S["o" + near], m_off)
        sent += write(T.mc, [c for c in here if c not in ports and topo.die(c) == my_die], T.mc, S.own,
                      _mask_of(_bits(m_on)[:N_OWN]))
        g.tensor.wait_ge(S.cp, 2)
        due = ["mc", other, near]
    else:
        g.wait_ge(S["o" + near], n_off)
        sent += write(T["r" + near], [p for p in ports if topo.die(p) == my_die], T["r" + near], S["o" + near], m_off | m_on)
        due = [near, "mc", other]

    g.tensor.wait_ge(S.lx, 16)
    for i, m in enumerate(due):
        if m == "mc":
            if not is_port:
                g.tensor.wait_ge(S.own, N_OWN)
            mat = T.mc
        else:
            g.tensor.wait_ge(S["o" + m], n_off + n_on if is_port and m == near else n_off)
            mat = T["r" + m]
        mmul = g.tensor.matmul(T.py[:, 0:64], mat[:, :], T.xs[:, :], i == 0, i == len(due) - 1)
    mmul.then_inc(S.my, 1)
    g.vector.wait_ge(S.my, 1)
    g.vector.tensor_copy(T.ys[:, :], T.py[:, 0:64]).then_inc(S.cy, 1)
    g.sync.wait_ge(S.cy, 1)
    g.sync.dma_start(T.y[:, :], T.ys[:, :]).then_inc(S.st, 16)
    g.sync.wait_ge(S.st, 16)
    g.wait_ge(S.snt, sent)
